import numpy as np
import ml_dtypes


def mxq(x, axis, fmt="e4m3"):
    dtype, down = {"e4m3": (ml_dtypes.float8_e4m3fn, 7), "e5m2": (ml_dtypes.float8_e5m2, 14)}[fmt]
    v = np.moveaxis(np.asarray(x, np.float32).astype(ml_dtypes.bfloat16).astype(np.float64), axis, -1)
    blocks = v.reshape(v.shape[:-1] + (-1, 32))
    amax = np.abs(blocks).max(-1, keepdims=True)
    byte = np.maximum(np.where(amax > 0, np.frexp(amax)[1] - 1 + 127, 0) - down, 1)
    scale = np.exp2(byte - 127.0)
    codes = (blocks / scale).astype(np.float32).astype(dtype).astype(np.float64)
    return np.moveaxis((codes * scale).reshape(v.shape), -1, axis)


WIDE = False


def mx_kscale(k):
    if not WIDE:
        return np.ones(k)
    levels = np.array([10, -10, 5, -5, 0])
    if k % 512:
        return np.exp2(np.random.permutation(np.resize(levels, k // 32))).repeat(32)
    a = np.empty((k // 512, 16))
    for p in range(k // 512):
        a[p, :8] = np.random.permutation(np.resize(levels, 8))
        for g in range(8):
            far = levels[np.abs(levels - a[p, g]) >= 10]
            a[p, g + 8] = far[np.random.randint(len(far))]
    return np.exp2(a.ravel()).repeat(32)


def f64(x):
    return np.asarray(x).astype(np.float64)


def striped(idx):
    return np.tile(np.asarray(idx).reshape(-1, 16).T, (8, 1)).astype(np.uint16)


def unstriped(offs):
    return offs[:16].T.reshape(-1).astype(np.int64)


E2M1 = np.array([0.0, 0.5, 1.0, 1.5, 2.0, 3.0, 4.0, 6.0, -0.0, -0.5, -1.0, -1.5, -2.0, -3.0, -4.0, -6.0])


def pack_weight(w, fmt):
    k, n = w.shape
    w = f64(np.asarray(w, np.float32).astype(ml_dtypes.bfloat16)).reshape(k // 32, 32, n)
    amax = np.abs(w).max(1)
    if fmt == "e4m3":
        byte = np.frexp(amax)[1] - 1 + 127 - 7
    else:
        mant, ex = np.frexp(amax / 6.0)
        byte = np.where(mant > 0.5, ex, ex - 1) + 127
    byte = np.clip(np.where(amax > 0, byte, 1), 1, 254)
    scaled = (w * np.exp2(127.0 - byte)[:, None, :]).reshape(k, n).astype(np.float32)
    by_word = np.ascontiguousarray(scaled.reshape(k // 512, 128, 4, n).transpose(0, 1, 3, 2))
    if fmt == "e4m3":
        words = by_word.astype(ml_dtypes.float8_e4m3fn).view(np.uint8)
    else:
        c = by_word.astype(ml_dtypes.float4_e2m1fn).view(np.uint8) & 0xF
        words = (c[..., 0::2] | (c[..., 1::2] << 4)).reshape(k // 512, 128, 2 * n)
    return np.ascontiguousarray(words), np.ascontiguousarray(byte.astype(np.uint8).reshape(k // 512, 16, n))


def unpack_weight(words, scales, fmt):
    g, _, n = scales.shape
    words = np.ascontiguousarray(words).reshape(g, 128, n, -1)
    if fmt == "e4m3":
        vals = words.view(ml_dtypes.float8_e4m3fn).astype(np.float64)
    else:
        nib = np.empty((g, 128, n, 4), np.uint8)
        nib[..., 0::2] = words & 0xF
        nib[..., 1::2] = words >> 4
        vals = E2M1[nib]
    vals = vals * np.repeat(np.exp2(scales.astype(np.float64) - 127.0), 8, axis=1)[..., None]
    return vals.transpose(0, 1, 3, 2).reshape(g * 512, n)


def bf(x):
    return np.asarray(x, np.float32).astype(ml_dtypes.bfloat16)


def planes(Y):
    r, m = Y.shape
    b = f64(bf(Y)).reshape(r // 32, 32, m)
    amax = np.abs(b).max(1)
    byte = np.clip(np.where(amax > 0, np.frexp(amax)[1] - 1 + 127 - 7, 1), 1, 254)
    codes = (b * np.exp2(127.0 - byte)[:, None, :]).reshape(r, m).astype(np.float32).astype(ml_dtypes.float8_e4m3fn).view(np.uint8)
    words = codes.reshape(r // 512, 128, 4, m).transpose(0, 1, 3, 2)
    return np.ascontiguousarray(words), np.ascontiguousarray(byte.astype(np.uint8).reshape(r // 512, 16, m))


K, R, F, T, J, M = 512, 512, 512, 2048, 512, 256


def setup_inputs():
    n = np.random.standard_normal
    idx = np.random.permutation(T)[:J]
    idx2 = np.random.permutation(J)[:M]
    idx3 = np.random.permutation(J)[:M]
    fk = mx_kscale(K)
    fr = mx_kscale(R)
    dtabp = pack_weight(n((K, T)) / fk[:, None], "e4m3")
    tabp = pack_weight(n((K, T)) / fk[:, None], "e4m3")
    return {
        "dtab_words": dtabp[0],
        "dtab_scales": dtabp[1],
        "tab_words": tabp[0],
        "tab_scales": tabp[1],
        "w1": (n((K, R)) * 1 / np.sqrt(K) * fk[:, None]).astype(np.float32),
        "soft": (np.random.uniform(0.5, 1.5, (R, 1))).astype(np.float32),
        "rs": (np.random.uniform(0.5, 2.0, (R, 1)) * fr[:, None]).astype(np.float32),
        "wor": (n((R, F)) * 1 / np.sqrt(R) / fr[:, None]).astype(np.float32),
        "res": (n((F, M)) * 0.5).astype(np.float32),
        "offs": striped(idx),
        "offs2": striped(idx2),
        "offs3": striped(idx3),
    }


def reference(dtab_words, dtab_scales, tab_words, tab_scales, w1, soft, rs, wor, res, offs, offs2, offs3):
    idx = unstriped(offs)
    idx2 = unstriped(offs2)
    idx3 = unstriped(offs3)
    dtabu = unpack_weight(dtab_words, dtab_scales, "e4m3")
    tabu = unpack_weight(tab_words, tab_scales, "e4m3")
    w1q = mxq(f64(w1), 0, "e4m3")
    tabidxg = tabu[:, idx]
    a = w1q.T @ tabidxg
    dtabidxg = dtabu[:, idx]
    ta = w1q.T @ dtabidxg
    n2 = np.sqrt(np.square(a[:, idx2]) * np.square(a[:, idx3]) + f64(soft))
    tn2 = (ta[:, idx2] * a[:, idx2] * 2.0 * np.square(a[:, idx3]) + ta[:, idx3] * a[:, idx3] * 2.0 * np.square(a[:, idx2])) * 0.5 / n2
    tu1 = (ta[:, idx2] * a[:, idx3] + ta[:, idx3] * a[:, idx2] - tn2 * a[:, idx2] * a[:, idx3] / n2) / n2
    fo1 = tu1 * f64(rs)
    worq = mxq(f64(wor), 0, "e4m3")
    fo1q = mxq(fo1, 0, "e4m3")
    yo = worq.T @ fo1q
    y = yo + f64(res)
    words, scales = planes(y)
    return y, words, scales

@@ -1,0 +1,253 @@
+from contextlib import ExitStack
+
+import concourse.mybir as mybir
+
+K, R, F, T, J, M = 512, 512, 512, 2048, 512, 256
+FLOPS = 2 * (2 * K * R * J + R * F * M)
+
+F32 = mybir.dt.float32
+BF16 = mybir.dt.bfloat16
+I32 = mybir.dt.int32
+U32 = mybir.dt.uint32
+U16 = mybir.dt.uint16
+U8 = mybir.dt.uint8
+FP8X4 = mybir.dt.float8_e4m3fn_x4
+ACT = mybir.ActivationFunctionType
+MULT = mybir.AluOpType.mult
+ADD = mybir.AluOpType.add
+
+P = 128
+PACK = 4
+D_ROW = 4
+M_EARLY = 192
+M_LATE = M - M_EARLY
+
+
+def tile_attend_tlikeness_o_pl_kernel(tc, dtab_words, dtab_scales, tab_words, tab_scales, w1, soft, rs, wor, res,
+                                       offs, offs2, offs3, out_0, out_1, out_2):
+    nc = tc.nc
+    with ExitStack() as ctx:
+        sb = ctx.enter_context(tc.tile_pool(name="sb", bufs=1))
+        ps1 = ctx.enter_context(tc.psum_pool(name="ps1", bufs=5))
+        ps2 = ctx.enter_context(tc.psum_pool(name="ps2", bufs=1))
+
+        def tile(name, shape, dtype, tag=None):
+            return sb.tile(shape, dtype, name=name, tag=tag or name, align_bytes=64)
+
+        list1 = tile("list1", [P, J // 16], U16)
+        list2 = tile("list2", [P, M // 16], U16)
+        list3 = tile("list3", [P, M // 16], U16)
+        tab_s = tile("tab_s", [P, T], U8)
+        dtab_s = tile("dtab_s", [P, T], U8)
+        soft_sb = tile("soft_sb", [P, PACK], F32)
+        rs_sb = tile("rs_sb", [P, PACK], F32)
+        warm = tile("warm", [P, 1], F32, tag="tab_w")
+        warm2 = tile("warm2", [P, 1], F32, tag="dtab_w")
+
+        nc.gpsimd.memset(warm[:], 1.0)
+        nc.gpsimd.memset(tab_s[:].bitcast(I32), 0)
+        nc.gpsimd.memset(dtab_s[:].bitcast(I32), 0)
+
+        def words_view(words):
+            return words[0].rearrange("p n t -> p (n t)").bitcast(I32)
+
+        def load_scales(queue, dst, scales, row):
+            for q in range(4):
+                queue.dma_start(out=dst[32 * q + row : 32 * q + row + 4, :].bitcast(I32),
+                                in_=scales[0, 4 * q : 4 * q + 4, :].bitcast(I32))
+
+        def load_weight(name, w):
+            raw = tile(name, [P, PACK, 512], F32, tag="raw")
+            nc.sync.dma_start(out=raw[:], in_=w.rearrange("(p j) c -> p j c", j=PACK))
+            return raw
+
+        def deal(copy, dst, raw, h):
+            copy(dst[:].rearrange("p (t m j) -> p m j t", t=PACK, j=PACK)[:, 64 * h : 64 * (h + 1)],
+                 raw[:].rearrange("p j (m t) -> p m j t", t=PACK)[:, 64 * h : 64 * (h + 1)])
+
+        nc.sync.dma_start(out=list1[:], in_=offs)
+        w1_raw = load_weight("w1_raw", w1)
+        nc.sync.dma_start(out=list3[:], in_=offs3)
+        nc.sync.dma_start(out=list2[:], in_=offs2)
+        load_scales(nc.sync, tab_s, tab_scales, 0)
+        nc.scalar.activation(warm2[:], warm[:], ACT.Ln)
+        tab_w = tile("tab_w", [P, T], U32)
+        dtab_w = tile("dtab_w", [P, T], U32)
+        nc.sync.dma_start(out=tab_w[:].bitcast(I32), in_=words_view(tab_words))
+        nc.sync.dma_start(out=dtab_w[:].bitcast(I32), in_=words_view(dtab_words))
+        load_scales(nc.gpsimd, dtab_s, dtab_scales, D_ROW)
+        nc.gpsimd.dma_start(out=soft_sb[:], in_=soft.rearrange("(p t) o -> p (t o)", t=PACK))
+        nc.gpsimd.dma_start(out=rs_sb[:], in_=rs.rearrange("(p t) o -> p (t o)", t=PACK))
+
+        coef = tile("coef", [P, PACK], F32)
+        nc.gpsimd.tensor_tensor(coef[:], soft_sb[:], rs_sb[:], MULT)
+
+        g_tab_s = tile("g_tab_s", [P, J], U8)
+        g_tab_w = tile("g_tab_w", [P, J], U32)
+        g_dtab_w = tile("g_dtab_w", [P, J], U32)
+        nc.vector.tensor_copy(g_tab_s[:], tab_s[:].indirect(list1[:]))
+
+        w1_b = tile("w1_b", [P, R * PACK], BF16, tag="w1_b_then_res")
+        w1_q = tile("w1_q", [P, R], U32)
+        w1_s = tile("w1_s", [P, R], U8)
+        deal(nc.scalar.copy, w1_b, w1_raw, 0)
+        deal(nc.vector.tensor_copy, w1_b, w1_raw, 1)
+        nc.vector.quantize_mx(out=w1_q[:].bitcast(FP8X4), scales=w1_s[:], in_=w1_b[:])
+        wor_raw = load_weight("wor_raw", wor)
+        res_sb = tile("res_sb", [P, PACK, M], F32, tag="w1_b_then_res")
+        nc.sync.dma_start(out=res_sb[:], in_=res.rearrange("(p t) m -> p t m", t=PACK))
+
+        def first_layer(whole, t, words, scales, row, slots, copy):
+            cols = slice(t * P, (t + 1) * P)
+            acc = ps1.tile([P, slots.stop - slots.start], F32, name="acc1")
+            nc.tensor.matmul_mx(out=acc[:], lhsT=w1_q[:, cols].bitcast(FP8X4), lhsT_scale=w1_s[:, cols],
+                                rhs=words[:, slots].bitcast(FP8X4), rhs_scale=scales[row:P, slots],
+                                start=True, stop=True)
+            copy(whole[:, slots], acc[:])
+
+        a = [tile("a%d" % t, [P, J], F32) for t in range(PACK)]
+        ta = [tile("ta%d" % t, [P, J], F32) for t in range(PACK)]
+        for h in range(2):
+            nc.vector.tensor_copy(g_tab_w[:, 256 * h : 256 * (h + 1)],
+                                  tab_w[:].indirect(list1[:, 16 * h : 16 * (h + 1)]))
+        first_layer(a[0], 0, g_tab_w, g_tab_s, 0, slice(0, 256), nc.scalar.copy)
+        first_layer(a[0], 0, g_tab_w, g_tab_s, 0, slice(256, 512), nc.scalar.copy)
+        for t in range(1, PACK):
+            first_layer(a[t], t, g_tab_w, g_tab_s, 0, slice(0, J), nc.scalar.copy)
+        g_dtab_s = tile("g_dtab_s", [P, J], U8, tag="tab_w")
+        nc.vector.tensor_copy(g_dtab_s[:], dtab_s[:].indirect(list1[:]))
+
+        x = [tile("x0", [P, M], F32)[:]]
+        y = [tile("y0", [P, M], F32)[:]]
+        prod = [tile("prod%d" % t, [P, M], F32) for t in range(PACK)]
+        logv = tile("logv", [P, PACK, M], F32)
+
+        def product(t):
+            nc.vector.tensor_tensor(prod[t][:], x[t], y[t], MULT)
+
+        def log_norm(t):
+            nc.scalar.activation(sq[:, t, :], prod[t][:], ACT.Square)
+            nc.scalar.activation(logv[:, t, :], sq[:, t, :], ACT.Ln, bias=soft_sb[:, t : t + 1])
+
+        for t in range(PACK):
+            nc.vector.tensor_copy(y[t], a[t][:].indirect(list3[:]))
+            if t > 0:
+                product(t - 1)
+            nc.vector.tensor_copy(x[t], a[t][:].indirect(list2[:]))
+            if t == 0:
+                nc.vector.tensor_copy(g_dtab_w[:], dtab_w[:].indirect(list1[:]))
+                rest = tile("rest", [P, 2, PACK - 1, M], F32, tag="dtab_w")
+                x.extend([rest[:, 0, u, :] for u in range(PACK - 1)])
+                y.extend([rest[:, 1, u, :] for u in range(PACK - 1)])
+                for u in range(PACK):
+                    first_layer(ta[u], u, g_dtab_w, g_dtab_s, D_ROW, slice(0, J), nc.scalar.copy)
+
+        sq = tile("sq", [P, PACK, M], F32, tag="g_dtab_w")
+        for t in range(PACK - 1):
+            log_norm(t)
+        wor_b = tile("wor_b", [P, F * PACK], BF16, tag="w1_q")
+        wor_q = tile("wor_q", [P, F], U32)
+        wor_s = tile("wor_s", [P, F], U8)
+
+        early, late = slice(0, M_EARLY), slice(M_EARLY, M)
+        spans = [early, late]
+        runs = [slice(0, 128), slice(128, M_EARLY), late]
+        t1 = [tile("t1_%d" % h, [P, PACK, s.stop - s.start], F32) for h, s in enumerate(spans)]
+        t2 = [tile("t2_0", [P, PACK, M_EARLY], F32)]
+        dp = [tile("dp_%d" % h, [P, PACK, s.stop - s.start], F32) for h, s in enumerate(spans)]
+        wgt = tile("wgt", [P, PACK, M], F32)
+        wc = tile("wc", [P, PACK, M], F32)
+        fo_b = tile("fo_b", [P, M * PACK], BF16)
+        fo_q = tile("fo_q", [P, M], U32)
+        fo_s = [tile("fo_s%d" % c, [P, s.stop - s.start], U8) for c, s in enumerate(runs)]
+        y_f = [tile("y_f%d" % h, [P, PACK, s.stop - s.start], F32) for h, s in enumerate(spans)]
+        y_b = tile("y_b", [P, M * PACK], BF16)
+        y_q = tile("y_q", [P, M], U32)
+        y_s = tile("y_s", [P, M], U8)
+        out_rows = out_0.rearrange("(p t) m -> p t m", t=PACK)
+        out_words = out_1[0].rearrange("p n t -> p (n t)").bitcast(I32)
+        walk = "p t (c i) -> p c t i"
+        woven = "p (c i t) -> p c t i"
+
+        def wide(s):
+            return slice(PACK * s.start, PACK * s.stop)
+
+        def term(dst, h, t, entries, other):
+            cols = spans[h]
+            part = slice(cols.start // 16, cols.stop // 16)
+            nc.vector.tensor_tensor(dst[h][:, t, :], ta[t][:].indirect(entries[:, part]), other[t][:, cols], MULT)
+
+        def tangents(h, t):
+            term(t1, h, t, list2, y)
+            term(t2, h, t, list3, x)
+
+        def weights():
+            nc.scalar.activation(wgt[:], logv[:], ACT.Exp, scale=-1.5)
+            for t in range(PACK):
+                nc.scalar.activation(wc[:, t, :], wgt[:, t, :], ACT.Copy, scale=coef[:, t : t + 1])
+
+        def sum_terms(h):
+            nc.vector.tensor_tensor(dp[h][:], t1[h][:], t2[h][:], ADD)
+
+        def weigh(h):
+            nc.vector.tensor_tensor(fo_b[:, wide(spans[h])].rearrange(woven, i=4, t=PACK),
+                                    dp[h][:].rearrange(walk, i=4), wc[:, :, spans[h]].rearrange(walk, i=4), MULT)
+
+        acc2 = []
+
+        def last_layer(c):
+            pairs = runs[c]
+            nc.vector.quantize_mx(out=fo_q[:, pairs].bitcast(FP8X4), scales=fo_s[c][:], in_=fo_b[:, wide(pairs)])
+            acc = ps2.tile([P, PACK, pairs.stop - pairs.start], F32, name="acc2_%d" % c)
+            for t in range(PACK):
+                cols = slice(t * P, (t + 1) * P)
+                nc.tensor.matmul_mx(out=acc[:, t, :], lhsT=wor_q[:, cols].bitcast(FP8X4), lhsT_scale=wor_s[:, cols],
+                                    rhs=fo_q[:, pairs].bitcast(FP8X4), rhs_scale=fo_s[c][:], start=True, stop=True)
+            acc2.append(acc)
+
+        def add_residual(c, copy):
+            pairs = runs[c]
+            h = 0 if pairs.start < M_EARLY else 1
+            mine = y_f[h][:, :, pairs.start - spans[h].start : pairs.stop - spans[h].start]
+            nc.vector.tensor_tensor(mine, acc2[c][:], res_sb[:, :, pairs], ADD)
+            copy(y_b[:, wide(pairs)].rearrange(woven, i=4, t=PACK), mine.rearrange(walk, i=4))
+
+        def store_y(h):
+            nc.sync.dma_start(out=out_rows[:, :, spans[h]], in_=y_f[h][:])
+
+        def quantise_y(pairs):
+            nc.vector.quantize_mx(out=y_q[:, pairs].bitcast(FP8X4), scales=y_s[:, pairs], in_=y_b[:, wide(pairs)])
+            nc.sync.dma_start(out=out_words[:, pairs], in_=y_q[:, pairs].bitcast(I32))
+
+        tangents(0, 0)
+        deal(nc.scalar.copy, wor_b, wor_raw, 0)
+        product(PACK - 1)
+        log_norm(PACK - 1)
+        weights()
+        deal(nc.scalar.copy, wor_b, wor_raw, 1)
+        for t in range(1, PACK):
+            tangents(0, t)
+        sum_terms(0)
+        for t in range(PACK):
+            term(t1, 1, t, list2, y)
+        weigh(0)
+        nc.vector.quantize_mx(out=wor_q[:].bitcast(FP8X4), scales=wor_s[:], in_=wor_b[:])
+        t2.append(tile("t2_1", [P, PACK, M_LATE], F32, tag="dp_0"))
+        last_layer(0)
+        last_layer(1)
+        for t in range(PACK):
+            term(t2, 1, t, list3, x)
+        add_residual(0, nc.scalar.copy)
+        sum_terms(1)
+        add_residual(1, nc.scalar.copy)
+        store_y(0)
+        weigh(1)
+        quantise_y(slice(0, 128))
+        last_layer(2)
+        add_residual(2, nc.vector.tensor_copy)
+        store_y(1)
+        quantise_y(slice(128, M))
+        for q in range(4):
+            queue = nc.scalar if q % 2 else nc.sync
+            queue.dma_start(out=out_2[0, 4 * q : 4 * q + 4, :].bitcast(I32),
+                            in_=y_s[32 * q : 32 * q + 4, :].bitcast(I32))

@@ -19,8 +19,8 @@ ADD = mybir.AluOpType.add
 P = 128
 PACK = 4
 D_ROW = 4
-M_EARLY = 192
-M_LATE = M - M_EARLY
+HALVES = 2
+MH = M // HALVES
 
 
 def tile_attend_tlikeness_o_pl_kernel(tc, dtab_words, dtab_scales, tab_words, tab_scales, w1, soft, rs, wor, res,
@@ -28,8 +28,8 @@ def tile_attend_tlikeness_o_pl_kernel(tc, dtab_words, dtab_scales, tab_words, ta
     nc = tc.nc
     with ExitStack() as ctx:
         sb = ctx.enter_context(tc.tile_pool(name="sb", bufs=1))
-        ps1 = ctx.enter_context(tc.psum_pool(name="ps1", bufs=5))
-        ps2 = ctx.enter_context(tc.psum_pool(name="ps2", bufs=1))
+        ps1 = ctx.enter_context(tc.psum_pool(name="ps1", bufs=6))
+        ps2 = ctx.enter_context(tc.psum_pool(name="ps2", bufs=2))
 
         def tile(name, shape, dtype, tag=None):
             return sb.tile(shape, dtype, name=name, tag=tag or name, align_bytes=64)
@@ -37,27 +37,27 @@ def tile_attend_tlikeness_o_pl_kernel(tc, dtab_words, dtab_scales, tab_words, ta
         list1 = tile("list1", [P, J // 16], U16)
         list2 = tile("list2", [P, M // 16], U16)
         list3 = tile("list3", [P, M // 16], U16)
-        tab_s = tile("tab_s", [P, T], U8)
-        dtab_s = tile("dtab_s", [P, T], U8)
+        tab_s = tile("tab_s", [P, T], U8, tag="dtab_w")
         soft_sb = tile("soft_sb", [P, PACK], F32)
         rs_sb = tile("rs_sb", [P, PACK], F32)
         warm = tile("warm", [P, 1], F32, tag="tab_w")
-        warm2 = tile("warm2", [P, 1], F32, tag="dtab_w")
+        warm2 = tile("warm2", [P, 1], F32, tag="dtab_s")
 
         nc.gpsimd.memset(warm[:], 1.0)
         nc.gpsimd.memset(tab_s[:].bitcast(I32), 0)
-        nc.gpsimd.memset(dtab_s[:].bitcast(I32), 0)
+        nc.gpsimd.dma_start(out=soft_sb[:], in_=soft.rearrange("(p t) o -> p (t o)", t=PACK))
+        nc.gpsimd.dma_start(out=rs_sb[:], in_=rs.rearrange("(p t) o -> p (t o)", t=PACK))
 
         def words_view(words):
             return words[0].rearrange("p n t -> p (n t)").bitcast(I32)
 
-        def load_scales(queue, dst, scales, row):
+        def load_scales(dst, scales, row):
             for q in range(4):
-                queue.dma_start(out=dst[32 * q + row : 32 * q + row + 4, :].bitcast(I32),
-                                in_=scales[0, 4 * q : 4 * q + 4, :].bitcast(I32))
+                nc.sync.dma_start(out=dst[32 * q + row : 32 * q + row + 4, :].bitcast(I32),
+                                  in_=scales[0, 4 * q : 4 * q + 4, :].bitcast(I32))
 
-        def load_weight(name, w):
-            raw = tile(name, [P, PACK, 512], F32, tag="raw")
+        def load_weight(name, w, tag):
+            raw = tile(name, [P, PACK, 512], F32, tag=tag)
             nc.sync.dma_start(out=raw[:], in_=w.rearrange("(p j) c -> p j c", j=PACK))
             return raw
 
@@ -66,18 +66,16 @@ def tile_attend_tlikeness_o_pl_kernel(tc, dtab_words, dtab_scales, tab_words, ta
                  raw[:].rearrange("p j (m t) -> p m j t", t=PACK)[:, 64 * h : 64 * (h + 1)])
 
         nc.sync.dma_start(out=list1[:], in_=offs)
-        w1_raw = load_weight("w1_raw", w1)
+        w1_raw = load_weight("w1_raw", w1, None)
         nc.sync.dma_start(out=list3[:], in_=offs3)
         nc.sync.dma_start(out=list2[:], in_=offs2)
-        load_scales(nc.sync, tab_s, tab_scales, 0)
+        load_scales(tab_s, tab_scales, 0)
         nc.scalar.activation(warm2[:], warm[:], ACT.Ln)
         tab_w = tile("tab_w", [P, T], U32)
-        dtab_w = tile("dtab_w", [P, T], U32)
+        dtab_s = tile("dtab_s", [P, T], U8)
         nc.sync.dma_start(out=tab_w[:].bitcast(I32), in_=words_view(tab_words))
-        nc.sync.dma_start(out=dtab_w[:].bitcast(I32), in_=words_view(dtab_words))
-        load_scales(nc.gpsimd, dtab_s, dtab_scales, D_ROW)
-        nc.gpsimd.dma_start(out=soft_sb[:], in_=soft.rearrange("(p t) o -> p (t o)", t=PACK))
-        nc.gpsimd.dma_start(out=rs_sb[:], in_=rs.rearrange("(p t) o -> p (t o)", t=PACK))
+        nc.vector.memset(dtab_s[:].bitcast(I32), 0)
+        load_scales(dtab_s, dtab_scales, D_ROW)
 
         coef = tile("coef", [P, PACK], F32)
         nc.gpsimd.tensor_tensor(coef[:], soft_sb[:], rs_sb[:], MULT)
@@ -86,34 +84,36 @@ def tile_attend_tlikeness_o_pl_kernel(tc, dtab_words, dtab_scales, tab_words, ta
         g_tab_w = tile("g_tab_w", [P, J], U32)
         g_dtab_w = tile("g_dtab_w", [P, J], U32)
         nc.vector.tensor_copy(g_tab_s[:], tab_s[:].indirect(list1[:]))
+        dtab_w = tile("dtab_w", [P, T], U32)
+        nc.sync.dma_start(out=dtab_w[:].bitcast(I32), in_=words_view(dtab_words))
 
-        w1_b = tile("w1_b", [P, R * PACK], BF16, tag="w1_b_then_res")
+        w1_b = tile("w1_b", [P, R * PACK], BF16)
         w1_q = tile("w1_q", [P, R], U32)
         w1_s = tile("w1_s", [P, R], U8)
         deal(nc.scalar.copy, w1_b, w1_raw, 0)
         deal(nc.vector.tensor_copy, w1_b, w1_raw, 1)
         nc.vector.quantize_mx(out=w1_q[:].bitcast(FP8X4), scales=w1_s[:], in_=w1_b[:])
-        wor_raw = load_weight("wor_raw", wor)
-        res_sb = tile("res_sb", [P, PACK, M], F32, tag="w1_b_then_res")
-        nc.sync.dma_start(out=res_sb[:], in_=res.rearrange("(p t) m -> p t m", t=PACK))
+        wor_raw = load_weight("wor_raw", wor, "w1_b")
 
-        def first_layer(whole, t, words, scales, row, slots, copy):
+        def first_layer(whole, t, words, scales, row, slots):
             cols = slice(t * P, (t + 1) * P)
             acc = ps1.tile([P, slots.stop - slots.start], F32, name="acc1")
             nc.tensor.matmul_mx(out=acc[:], lhsT=w1_q[:, cols].bitcast(FP8X4), lhsT_scale=w1_s[:, cols],
                                 rhs=words[:, slots].bitcast(FP8X4), rhs_scale=scales[row:P, slots],
                                 start=True, stop=True)
-            copy(whole[:, slots], acc[:])
+            nc.scalar.copy(whole[:, slots], acc[:])
 
         a = [tile("a%d" % t, [P, J], F32) for t in range(PACK)]
         ta = [tile("ta%d" % t, [P, J], F32) for t in range(PACK)]
         for h in range(2):
             nc.vector.tensor_copy(g_tab_w[:, 256 * h : 256 * (h + 1)],
                                   tab_w[:].indirect(list1[:, 16 * h : 16 * (h + 1)]))
-        first_layer(a[0], 0, g_tab_w, g_tab_s, 0, slice(0, 256), nc.scalar.copy)
-        first_layer(a[0], 0, g_tab_w, g_tab_s, 0, slice(256, 512), nc.scalar.copy)
+        first_layer(a[0], 0, g_tab_w, g_tab_s, 0, slice(0, 256))
+        first_layer(a[0], 0, g_tab_w, g_tab_s, 0, slice(256, 512))
         for t in range(1, PACK):
-            first_layer(a[t], t, g_tab_w, g_tab_s, 0, slice(0, J), nc.scalar.copy)
+            first_layer(a[t], t, g_tab_w, g_tab_s, 0, slice(0, J))
+        res_sb = tile("res_sb", [P, PACK, M], F32, tag="g_tab_w")
+        nc.sync.dma_start(out=res_sb[:], in_=res.rearrange("(p t) m -> p t m", t=PACK))
         g_dtab_s = tile("g_dtab_s", [P, J], U8, tag="tab_w")
         nc.vector.tensor_copy(g_dtab_s[:], dtab_s[:].indirect(list1[:]))
 
@@ -140,7 +140,7 @@ def tile_attend_tlikeness_o_pl_kernel(tc, dtab_words, dtab_scales, tab_words, ta
                 x.extend([rest[:, 0, u, :] for u in range(PACK - 1)])
                 y.extend([rest[:, 1, u, :] for u in range(PACK - 1)])
                 for u in range(PACK):
-                    first_layer(ta[u], u, g_dtab_w, g_dtab_s, D_ROW, slice(0, J), nc.scalar.copy)
+                    first_layer(ta[u], u, g_dtab_w, g_dtab_s, D_ROW, slice(0, J))
 
         sq = tile("sq", [P, PACK, M], F32, tag="g_dtab_w")
         for t in range(PACK - 1):
@@ -149,37 +149,27 @@ def tile_attend_tlikeness_o_pl_kernel(tc, dtab_words, dtab_scales, tab_words, ta
         wor_q = tile("wor_q", [P, F], U32)
         wor_s = tile("wor_s", [P, F], U8)
 
-        early, late = slice(0, M_EARLY), slice(M_EARLY, M)
-        spans = [early, late]
-        runs = [slice(0, 128), slice(128, M_EARLY), late]
-        t1 = [tile("t1_%d" % h, [P, PACK, s.stop - s.start], F32) for h, s in enumerate(spans)]
-        t2 = [tile("t2_0", [P, PACK, M_EARLY], F32)]
-        dp = [tile("dp_%d" % h, [P, PACK, s.stop - s.start], F32) for h, s in enumerate(spans)]
+        halves = [slice(h * MH, (h + 1) * MH) for h in range(HALVES)]
+        t1 = tile("t1", [P, PACK, M], F32)
+        t2 = tile("t2", [P, PACK, M], F32)
         wgt = tile("wgt", [P, PACK, M], F32)
         wc = tile("wc", [P, PACK, M], F32)
-        fo_b = tile("fo_b", [P, M * PACK], BF16)
-        fo_q = tile("fo_q", [P, M], U32)
-        fo_s = [tile("fo_s%d" % c, [P, s.stop - s.start], U8) for c, s in enumerate(runs)]
-        y_f = [tile("y_f%d" % h, [P, PACK, s.stop - s.start], F32) for h, s in enumerate(spans)]
-        y_b = tile("y_b", [P, M * PACK], BF16)
-        y_q = tile("y_q", [P, M], U32)
+        dp = [tile("dp%d" % h, [P, PACK, MH], F32) for h in range(HALVES)]
+        fo_b = [tile("fo_b%d" % h, [P, MH * PACK], BF16) for h in range(HALVES)]
+        fo_q = [tile("fo_q%d" % h, [P, MH], U32) for h in range(HALVES)]
+        fo_s = [tile("fo_s%d" % h, [P, MH], U8) for h in range(HALVES)]
+        y_f = [tile("y_f%d" % h, [P, PACK, MH], F32) for h in range(HALVES)]
+        y_b = [tile("y_b%d" % h, [P, MH * PACK], BF16) for h in range(HALVES)]
+        y_q = [tile("y_q%d" % h, [P, MH], U32) for h in range(HALVES)]
         y_s = tile("y_s", [P, M], U8)
         out_rows = out_0.rearrange("(p t) m -> p t m", t=PACK)
         out_words = out_1[0].rearrange("p n t -> p (n t)").bitcast(I32)
         walk = "p t (c i) -> p c t i"
         woven = "p (c i t) -> p c t i"
 
-        def wide(s):
-            return slice(PACK * s.start, PACK * s.stop)
-
-        def term(dst, h, t, entries, other):
-            cols = spans[h]
-            part = slice(cols.start // 16, cols.stop // 16)
-            nc.vector.tensor_tensor(dst[h][:, t, :], ta[t][:].indirect(entries[:, part]), other[t][:, cols], MULT)
-
-        def tangents(h, t):
-            term(t1, h, t, list2, y)
-            term(t2, h, t, list3, x)
+        def tangents(t):
+            nc.vector.tensor_tensor(t1[:, t, :], ta[t][:].indirect(list2[:]), y[t], MULT)
+            nc.vector.tensor_tensor(t2[:, t, :], ta[t][:].indirect(list3[:]), x[t], MULT)
 
         def weights():
             nc.scalar.activation(wgt[:], logv[:], ACT.Exp, scale=-1.5)
@@ -187,66 +177,51 @@ def tile_attend_tlikeness_o_pl_kernel(tc, dtab_words, dtab_scales, tab_words, ta
                 nc.scalar.activation(wc[:, t, :], wgt[:, t, :], ACT.Copy, scale=coef[:, t : t + 1])
 
         def sum_terms(h):
-            nc.vector.tensor_tensor(dp[h][:], t1[h][:], t2[h][:], ADD)
+            nc.vector.tensor_tensor(dp[h][:], t1[:, :, halves[h]], t2[:, :, halves[h]], ADD)
 
         def weigh(h):
-            nc.vector.tensor_tensor(fo_b[:, wide(spans[h])].rearrange(woven, i=4, t=PACK),
-                                    dp[h][:].rearrange(walk, i=4), wc[:, :, spans[h]].rearrange(walk, i=4), MULT)
+            nc.vector.tensor_tensor(fo_b[h][:].rearrange(woven, i=4, t=PACK),
+                                    dp[h][:].rearrange(walk, i=4), wc[:, :, halves[h]].rearrange(walk, i=4), MULT)
 
         acc2 = []
 
-        def last_layer(c):
-            pairs = runs[c]
-            nc.vector.quantize_mx(out=fo_q[:, pairs].bitcast(FP8X4), scales=fo_s[c][:], in_=fo_b[:, wide(pairs)])
-            acc = ps2.tile([P, PACK, pairs.stop - pairs.start], F32, name="acc2_%d" % c)
+        def last_layer(h):
+            nc.vector.quantize_mx(out=fo_q[h][:].bitcast(FP8X4), scales=fo_s[h][:], in_=fo_b[h][:])
+            acc = ps2.tile([P, PACK, MH], F32, name="acc2")
             for t in range(PACK):
                 cols = slice(t * P, (t + 1) * P)
                 nc.tensor.matmul_mx(out=acc[:, t, :], lhsT=wor_q[:, cols].bitcast(FP8X4), lhsT_scale=wor_s[:, cols],
-                                    rhs=fo_q[:, pairs].bitcast(FP8X4), rhs_scale=fo_s[c][:], start=True, stop=True)
+                                    rhs=fo_q[h][:].bitcast(FP8X4), rhs_scale=fo_s[h][:], start=True, stop=True)
             acc2.append(acc)
 
-        def add_residual(c, copy):
-            pairs = runs[c]
-            h = 0 if pairs.start < M_EARLY else 1
-            mine = y_f[h][:, :, pairs.start - spans[h].start : pairs.stop - spans[h].start]
-            nc.vector.tensor_tensor(mine, acc2[c][:], res_sb[:, :, pairs], ADD)
-            copy(y_b[:, wide(pairs)].rearrange(woven, i=4, t=PACK), mine.rearrange(walk, i=4))
+        def add_residual(h, copy):
+            nc.vector.tensor_tensor(y_f[h][:], acc2[h][:], res_sb[:, :, halves[h]], ADD)
+            nc.sync.dma_start(out=out_rows[:, :, halves[h]], in_=y_f[h][:])
+            copy(y_b[h][:].rearrange(woven, i=4, t=PACK), y_f[h][:].rearrange(walk, i=4))
 
-        def store_y(h):
-            nc.sync.dma_start(out=out_rows[:, :, spans[h]], in_=y_f[h][:])
+        def quantise_y(h):
+            nc.vector.quantize_mx(out=y_q[h][:].bitcast(FP8X4), scales=y_s[:, halves[h]], in_=y_b[h][:])
+            nc.sync.dma_start(out=out_words[:, halves[h]], in_=y_q[h][:].bitcast(I32))
 
-        def quantise_y(pairs):
-            nc.vector.quantize_mx(out=y_q[:, pairs].bitcast(FP8X4), scales=y_s[:, pairs], in_=y_b[:, wide(pairs)])
-            nc.sync.dma_start(out=out_words[:, pairs], in_=y_q[:, pairs].bitcast(I32))
-
-        tangents(0, 0)
+        tangents(0)
         deal(nc.scalar.copy, wor_b, wor_raw, 0)
         product(PACK - 1)
         log_norm(PACK - 1)
-        weights()
         deal(nc.scalar.copy, wor_b, wor_raw, 1)
+        weights()
         for t in range(1, PACK):
-            tangents(0, t)
-        sum_terms(0)
-        for t in range(PACK):
-            term(t1, 1, t, list2, y)
-        weigh(0)
+            tangents(t)
         nc.vector.quantize_mx(out=wor_q[:].bitcast(FP8X4), scales=wor_s[:], in_=wor_b[:])
-        t2.append(tile("t2_1", [P, PACK, M_LATE], F32, tag="dp_0"))
-        last_layer(0)
-        last_layer(1)
-        for t in range(PACK):
-            term(t2, 1, t, list3, x)
-        add_residual(0, nc.scalar.copy)
+        sum_terms(0)
         sum_terms(1)
-        add_residual(1, nc.scalar.copy)
-        store_y(0)
+        weigh(0)
+        last_layer(0)
         weigh(1)
-        quantise_y(slice(0, 128))
-        last_layer(2)
-        add_residual(2, nc.vector.tensor_copy)
-        store_y(1)
-        quantise_y(slice(128, M))
+        last_layer(1)
+        add_residual(0, nc.scalar.copy)
+        add_residual(1, nc.vector.tensor_copy)
+        quantise_y(0)
+        quantise_y(1)
         for q in range(4):
             queue = nc.scalar if q % 2 else nc.sync
             queue.dma_start(out=out_2[0, 4 * q : 4 * q + 4, :].bitcast(I32),

@@ -18,9 +18,14 @@ ADD = mybir.AluOpType.add
 
 P = 128
 PACK = 4
-D_ROW = 4
+QUADS = 4
+PER_COLUMN = 16
+DTAB_ROW = 4
+W1_ON_SCALAR = 96
 HALVES = 2
 MH = M // HALVES
+LINE = 4
+FIRST_LAYER_BANKS = 6
 
 
 def tile_attend_tlikeness_o_pl_kernel(tc, dtab_words, dtab_scales, tab_words, tab_scales, w1, soft, rs, wor, res,
@@ -28,54 +33,59 @@ def tile_attend_tlikeness_o_pl_kernel(tc, dtab_words, dtab_scales, tab_words, ta
     nc = tc.nc
     with ExitStack() as ctx:
         sb = ctx.enter_context(tc.tile_pool(name="sb", bufs=1))
-        ps1 = ctx.enter_context(tc.psum_pool(name="ps1", bufs=6))
-        ps2 = ctx.enter_context(tc.psum_pool(name="ps2", bufs=2))
+        ps1 = ctx.enter_context(tc.psum_pool(name="ps1", bufs=FIRST_LAYER_BANKS))
+        ps2 = ctx.enter_context(tc.psum_pool(name="ps2", bufs=HALVES))
+        tag_of = {}
 
-        def tile(name, shape, dtype, tag=None):
-            return sb.tile(shape, dtype, name=name, tag=tag or name, align_bytes=64)
-
-        list1 = tile("list1", [P, J // 16], U16)
-        list2 = tile("list2", [P, M // 16], U16)
-        list3 = tile("list3", [P, M // 16], U16)
-        tab_s = tile("tab_s", [P, T], U8, tag="dtab_w")
-        soft_sb = tile("soft_sb", [P, PACK], F32)
-        rs_sb = tile("rs_sb", [P, PACK], F32)
-        warm = tile("warm", [P, 1], F32, tag="tab_w")
-        warm2 = tile("warm2", [P, 1], F32, tag="dtab_s")
-
-        nc.gpsimd.memset(warm[:], 1.0)
-        nc.gpsimd.memset(tab_s[:].bitcast(I32), 0)
-        nc.gpsimd.dma_start(out=soft_sb[:], in_=soft.rearrange("(p t) o -> p (t o)", t=PACK))
-        nc.gpsimd.dma_start(out=rs_sb[:], in_=rs.rearrange("(p t) o -> p (t o)", t=PACK))
+        def tile(name, shape, dtype, after=None):
+            tag = tag_of.get(after, name)
+            tag_of.setdefault(name, tag)
+            return sb.tile(shape, dtype, name=name, tag=tag, align_bytes=64)
 
         def words_view(words):
             return words[0].rearrange("p n t -> p (n t)").bitcast(I32)
 
         def load_scales(dst, scales, row):
-            for q in range(4):
-                nc.sync.dma_start(out=dst[32 * q + row : 32 * q + row + 4, :].bitcast(I32),
-                                  in_=scales[0, 4 * q : 4 * q + 4, :].bitcast(I32))
+            for q in range(QUADS):
+                nc.sync.dma_start(out=dst[32 * q + row : 32 * q + row + PACK, :].bitcast(I32),
+                                  in_=scales[0, PACK * q : PACK * (q + 1), :].bitcast(I32))
 
-        def load_weight(name, w, tag):
-            raw = tile(name, [P, PACK, 512], F32, tag=tag)
-            nc.sync.dma_start(out=raw[:], in_=w.rearrange("(p j) c -> p j c", j=PACK))
+        def load_weight(name, weight, after=None):
+            raw = tile(name, [P, PACK, weight.shape[1]], F32, after)
+            nc.sync.dma_start(out=raw[:], in_=weight.rearrange("(p j) c -> p j c", j=PACK))
             return raw
 
-        def deal(copy, dst, raw, h):
-            copy(dst[:].rearrange("p (t m j) -> p m j t", t=PACK, j=PACK)[:, 64 * h : 64 * (h + 1)],
-                 raw[:].rearrange("p j (m t) -> p m j t", t=PACK)[:, 64 * h : 64 * (h + 1)])
+        def deal(copy, dst, raw, groups):
+            copy(dst[:].rearrange("p (t i j) -> p i j t", t=PACK, j=PACK)[:, groups],
+                 raw[:].rearrange("p j (i t) -> p i j t", t=PACK)[:, groups])
+
+        list1 = tile("list1", [P, J // PER_COLUMN], U16)
+        list2 = tile("list2", [P, M // PER_COLUMN], U16)
+        list3 = tile("list3", [P, M // PER_COLUMN], U16)
+        tab_s = tile("tab_s", [P, T], U8)
+        soft_sb = tile("soft_sb", [P, PACK], F32)
+        rs_sb = tile("rs_sb", [P, PACK], F32)
+        ln_in = tile("ln_in", [P, 1], F32)
+        ln_bias = tile("ln_bias", [P, 1], F32)
+        zero = tile("zero", [P, 1], F32)
+
+        nc.gpsimd.memset(ln_in[:], 0.0)
+        nc.gpsimd.memset(ln_bias[:], 1.0)
+        nc.gpsimd.memset(tab_s[:].bitcast(I32), 0)
+        nc.gpsimd.dma_start(out=soft_sb[:], in_=soft.rearrange("(p t) o -> p (t o)", t=PACK))
+        nc.gpsimd.dma_start(out=rs_sb[:], in_=rs.rearrange("(p t) o -> p (t o)", t=PACK))
 
         nc.sync.dma_start(out=list1[:], in_=offs)
-        w1_raw = load_weight("w1_raw", w1, None)
+        w1_raw = load_weight("w1_raw", w1)
         nc.sync.dma_start(out=list3[:], in_=offs3)
         nc.sync.dma_start(out=list2[:], in_=offs2)
         load_scales(tab_s, tab_scales, 0)
-        nc.scalar.activation(warm2[:], warm[:], ACT.Ln)
-        tab_w = tile("tab_w", [P, T], U32)
-        dtab_s = tile("dtab_s", [P, T], U8)
+        nc.scalar.activation(zero[:], ln_in[:], ACT.Ln, bias=ln_bias[:])
+        tab_w = tile("tab_w", [P, T], U32, after="ln_in")
+        dtab_s = tile("dtab_s", [P, T], U8, after="ln_bias")
         nc.sync.dma_start(out=tab_w[:].bitcast(I32), in_=words_view(tab_words))
         nc.vector.memset(dtab_s[:].bitcast(I32), 0)
-        load_scales(dtab_s, dtab_scales, D_ROW)
+        load_scales(dtab_s, dtab_scales, DTAB_ROW)
 
         coef = tile("coef", [P, PACK], F32)
         nc.gpsimd.tensor_tensor(coef[:], soft_sb[:], rs_sb[:], MULT)
@@ -84,16 +94,16 @@ def tile_attend_tlikeness_o_pl_kernel(tc, dtab_words, dtab_scales, tab_words, ta
         g_tab_w = tile("g_tab_w", [P, J], U32)
         g_dtab_w = tile("g_dtab_w", [P, J], U32)
         nc.vector.tensor_copy(g_tab_s[:], tab_s[:].indirect(list1[:]))
-        dtab_w = tile("dtab_w", [P, T], U32)
-        nc.sync.dma_start(out=dtab_w[:].bitcast(I32), in_=words_view(dtab_words))
 
         w1_b = tile("w1_b", [P, R * PACK], BF16)
         w1_q = tile("w1_q", [P, R], U32)
-        w1_s = tile("w1_s", [P, R], U8)
-        deal(nc.scalar.copy, w1_b, w1_raw, 0)
-        deal(nc.vector.tensor_copy, w1_b, w1_raw, 1)
+        w1_s = tile("w1_s", [P, R], U8, after="tab_s")
+        deal(nc.scalar.copy, w1_b, w1_raw, slice(0, W1_ON_SCALAR))
+        deal(nc.vector.tensor_copy, w1_b, w1_raw, slice(W1_ON_SCALAR, P))
+        dtab_w = tile("dtab_w", [P, T], U32, after="w1_raw")
+        nc.sync.dma_start(out=dtab_w[:].bitcast(I32), in_=words_view(dtab_words))
         nc.vector.quantize_mx(out=w1_q[:].bitcast(FP8X4), scales=w1_s[:], in_=w1_b[:])
-        wor_raw = load_weight("wor_raw", wor, "w1_b")
+        wor_raw = load_weight("wor_raw", wor, after="w1_b")
 
         def first_layer(whole, t, words, scales, row, slots):
             cols = slice(t * P, (t + 1) * P)
@@ -105,124 +115,131 @@ def tile_attend_tlikeness_o_pl_kernel(tc, dtab_words, dtab_scales, tab_words, ta
 
         a = [tile("a%d" % t, [P, J], F32) for t in range(PACK)]
         ta = [tile("ta%d" % t, [P, J], F32) for t in range(PACK)]
-        for h in range(2):
-            nc.vector.tensor_copy(g_tab_w[:, 256 * h : 256 * (h + 1)],
-                                  tab_w[:].indirect(list1[:, 16 * h : 16 * (h + 1)]))
-        first_layer(a[0], 0, g_tab_w, g_tab_s, 0, slice(0, 256))
-        first_layer(a[0], 0, g_tab_w, g_tab_s, 0, slice(256, 512))
+        slot_halves = [slice(0, J // 2), slice(J // 2, J)]
+        for slots in slot_halves:
+            entries = slice(slots.start // PER_COLUMN, slots.stop // PER_COLUMN)
+            nc.vector.tensor_copy(g_tab_w[:, slots], tab_w[:].indirect(list1[:, entries]))
+        for slots in slot_halves:
+            first_layer(a[0], 0, g_tab_w, g_tab_s, 0, slots)
         for t in range(1, PACK):
             first_layer(a[t], t, g_tab_w, g_tab_s, 0, slice(0, J))
-        res_sb = tile("res_sb", [P, PACK, M], F32, tag="g_tab_w")
+        res_sb = tile("res_sb", [P, PACK, M], F32, after="g_tab_w")
         nc.sync.dma_start(out=res_sb[:], in_=res.rearrange("(p t) m -> p t m", t=PACK))
-        g_dtab_s = tile("g_dtab_s", [P, J], U8, tag="tab_w")
+        g_dtab_s = tile("g_dtab_s", [P, J], U8, after="tab_w")
         nc.vector.tensor_copy(g_dtab_s[:], dtab_s[:].indirect(list1[:]))
 
-        x = [tile("x0", [P, M], F32)[:]]
-        y = [tile("y0", [P, M], F32)[:]]
+        last = PACK - 1
+        uv_first = tile("uv_first", [P, 2, M], F32, after="dtab_s")
+        u = [uv_first[:, 0, :]]
+        v = [uv_first[:, 1, :]]
+        square = [tile("square_first", [P, M], F32, after="g_tab_s")[:]]
         prod = [tile("prod%d" % t, [P, M], F32) for t in range(PACK)]
-        logv = tile("logv", [P, PACK, M], F32)
+        log_n2sq = tile("log_n2sq", [P, PACK, M], F32)
 
-        def product(t):
-            nc.vector.tensor_tensor(prod[t][:], x[t], y[t], MULT)
+        def look_up(t):
+            nc.vector.tensor_copy(v[t], a[t][:].indirect(list3[:]))
+            nc.vector.tensor_copy(u[t], a[t][:].indirect(list2[:]))
+
+        def product(t, engine):
+            engine.tensor_tensor(prod[t][:], u[t], v[t], MULT)
 
         def log_norm(t):
-            nc.scalar.activation(sq[:, t, :], prod[t][:], ACT.Square)
-            nc.scalar.activation(logv[:, t, :], sq[:, t, :], ACT.Ln, bias=soft_sb[:, t : t + 1])
+            nc.scalar.activation(square[t], prod[t][:], ACT.Square)
+            nc.scalar.activation(log_n2sq[:, t, :], square[t], ACT.Ln, bias=soft_sb[:, t : t + 1])
 
+        look_up(0)
+        product(0, nc.gpsimd)
+        nc.vector.tensor_copy(g_dtab_w[:], dtab_w[:].indirect(list1[:]))
+        uv_rest = tile("uv_rest", [P, 2, last, M], F32, after="dtab_w")
+        u.extend([uv_rest[:, 0, i, :] for i in range(last)])
+        v.extend([uv_rest[:, 1, i, :] for i in range(last)])
         for t in range(PACK):
-            nc.vector.tensor_copy(y[t], a[t][:].indirect(list3[:]))
-            if t > 0:
-                product(t - 1)
-            nc.vector.tensor_copy(x[t], a[t][:].indirect(list2[:]))
-            if t == 0:
-                nc.vector.tensor_copy(g_dtab_w[:], dtab_w[:].indirect(list1[:]))
-                rest = tile("rest", [P, 2, PACK - 1, M], F32, tag="dtab_w")
-                x.extend([rest[:, 0, u, :] for u in range(PACK - 1)])
-                y.extend([rest[:, 1, u, :] for u in range(PACK - 1)])
-                for u in range(PACK):
-                    first_layer(ta[u], u, g_dtab_w, g_dtab_s, D_ROW, slice(0, J))
+            first_layer(ta[t], t, g_dtab_w, g_dtab_s, DTAB_ROW, slice(0, J))
+        for t in range(1, last):
+            look_up(t)
+            product(t, nc.gpsimd)
+        look_up(last)
 
-        sq = tile("sq", [P, PACK, M], F32, tag="g_dtab_w")
-        for t in range(PACK - 1):
+        square_rest = tile("square_rest", [P, last, M], F32, after="g_dtab_w")
+        square.extend([square_rest[:, i, :] for i in range(last)])
+        for t in range(last):
             log_norm(t)
-        wor_b = tile("wor_b", [P, F * PACK], BF16, tag="w1_q")
+        wor_b = tile("wor_b", [P, F * PACK], BF16, after="w1_q")
         wor_q = tile("wor_q", [P, F], U32)
         wor_s = tile("wor_s", [P, F], U8)
 
         halves = [slice(h * MH, (h + 1) * MH) for h in range(HALVES)]
-        t1 = tile("t1", [P, PACK, M], F32)
-        t2 = tile("t2", [P, PACK, M], F32)
-        wgt = tile("wgt", [P, PACK, M], F32)
-        wc = tile("wc", [P, PACK, M], F32)
-        dp = [tile("dp%d" % h, [P, PACK, MH], F32) for h in range(HALVES)]
+        du_v = tile("du_v", [P, PACK, M], F32)
+        dv_u = tile("dv_u", [P, PACK, M], F32)
+        power = tile("power", [P, PACK, M], F32)
+        factor = tile("factor", [P, PACK, M], F32)
+        dprod = [tile("dprod%d" % h, [P, PACK, MH], F32) for h in range(HALVES)]
         fo_b = [tile("fo_b%d" % h, [P, MH * PACK], BF16) for h in range(HALVES)]
         fo_q = [tile("fo_q%d" % h, [P, MH], U32) for h in range(HALVES)]
         fo_s = [tile("fo_s%d" % h, [P, MH], U8) for h in range(HALVES)]
-        y_f = [tile("y_f%d" % h, [P, PACK, MH], F32) for h in range(HALVES)]
-        y_b = [tile("y_b%d" % h, [P, MH * PACK], BF16) for h in range(HALVES)]
-        y_q = [tile("y_q%d" % h, [P, MH], U32) for h in range(HALVES)]
-        y_s = tile("y_s", [P, M], U8)
+        out_f = [tile("out_f%d" % h, [P, PACK, MH], F32) for h in range(HALVES)]
+        out_b = [tile("out_b%d" % h, [P, MH * PACK], BF16) for h in range(HALVES)]
+        out_q = [tile("out_q%d" % h, [P, MH], U32) for h in range(HALVES)]
+        out_s = tile("out_s", [P, M], U8)
         out_rows = out_0.rearrange("(p t) m -> p t m", t=PACK)
-        out_words = out_1[0].rearrange("p n t -> p (n t)").bitcast(I32)
-        walk = "p t (c i) -> p c t i"
-        woven = "p (c i t) -> p c t i"
+        out_words = words_view(out_1)
+
+        def by_tile(ap):
+            return ap.rearrange("p t (c i) -> p c t i", i=LINE)
+
+        def woven(ap):
+            return ap.rearrange("p (c i t) -> p c t i", i=LINE, t=PACK)
 
         def tangents(t):
-            nc.vector.tensor_tensor(t1[:, t, :], ta[t][:].indirect(list2[:]), y[t], MULT)
-            nc.vector.tensor_tensor(t2[:, t, :], ta[t][:].indirect(list3[:]), x[t], MULT)
+            nc.vector.tensor_tensor(du_v[:, t, :], ta[t][:].indirect(list2[:]), v[t], MULT)
+            nc.vector.tensor_tensor(dv_u[:, t, :], ta[t][:].indirect(list3[:]), u[t], MULT)
 
-        def weights():
-            nc.scalar.activation(wgt[:], logv[:], ACT.Exp, scale=-1.5)
+        def factors(h):
+            nc.scalar.activation(power[:, :, halves[h]], log_n2sq[:, :, halves[h]], ACT.Exp, bias=zero[:], scale=-1.5)
             for t in range(PACK):
-                nc.scalar.activation(wc[:, t, :], wgt[:, t, :], ACT.Copy, scale=coef[:, t : t + 1])
+                nc.scalar.activation(factor[:, t, halves[h]], power[:, t, halves[h]], ACT.Copy,
+                                     scale=coef[:, t : t + 1])
 
         def sum_terms(h):
-            nc.vector.tensor_tensor(dp[h][:], t1[:, :, halves[h]], t2[:, :, halves[h]], ADD)
-
-        def weigh(h):
-            nc.vector.tensor_tensor(fo_b[h][:].rearrange(woven, i=4, t=PACK),
-                                    dp[h][:].rearrange(walk, i=4), wc[:, :, halves[h]].rearrange(walk, i=4), MULT)
-
-        acc2 = []
+            nc.vector.tensor_tensor(dprod[h][:], du_v[:, :, halves[h]], dv_u[:, :, halves[h]], ADD)
 
         def last_layer(h):
+            nc.vector.tensor_tensor(woven(fo_b[h][:]), by_tile(dprod[h][:]), by_tile(factor[:, :, halves[h]]), MULT)
             nc.vector.quantize_mx(out=fo_q[h][:].bitcast(FP8X4), scales=fo_s[h][:], in_=fo_b[h][:])
             acc = ps2.tile([P, PACK, MH], F32, name="acc2")
             for t in range(PACK):
                 cols = slice(t * P, (t + 1) * P)
                 nc.tensor.matmul_mx(out=acc[:, t, :], lhsT=wor_q[:, cols].bitcast(FP8X4), lhsT_scale=wor_s[:, cols],
                                     rhs=fo_q[h][:].bitcast(FP8X4), rhs_scale=fo_s[h][:], start=True, stop=True)
-            acc2.append(acc)
+            return acc
 
-        def add_residual(h, copy):
-            nc.vector.tensor_tensor(y_f[h][:], acc2[h][:], res_sb[:, :, halves[h]], ADD)
-            nc.sync.dma_start(out=out_rows[:, :, halves[h]], in_=y_f[h][:])
-            copy(y_b[h][:].rearrange(woven, i=4, t=PACK), y_f[h][:].rearrange(walk, i=4))
+        def add_residual(h, acc, copy):
+            nc.vector.tensor_tensor(out_f[h][:], acc[:], res_sb[:, :, halves[h]], ADD)
+            nc.sync.dma_start(out=out_rows[:, :, halves[h]], in_=out_f[h][:])
+            copy(woven(out_b[h][:]), by_tile(out_f[h][:]))
 
-        def quantise_y(h):
-            nc.vector.quantize_mx(out=y_q[h][:].bitcast(FP8X4), scales=y_s[:, halves[h]], in_=y_b[h][:])
-            nc.sync.dma_start(out=out_words[:, halves[h]], in_=y_q[h][:].bitcast(I32))
+        def quantise_out(h):
+            nc.vector.quantize_mx(out=out_q[h][:].bitcast(FP8X4), scales=out_s[:, halves[h]], in_=out_b[h][:])
+            nc.sync.dma_start(out=out_words[:, halves[h]], in_=out_q[h][:].bitcast(I32))
 
         tangents(0)
-        deal(nc.scalar.copy, wor_b, wor_raw, 0)
-        product(PACK - 1)
-        log_norm(PACK - 1)
-        deal(nc.scalar.copy, wor_b, wor_raw, 1)
-        weights()
+        deal(nc.scalar.copy, wor_b, wor_raw, slice(0, P // 2))
+        product(last, nc.vector)
+        log_norm(last)
+        deal(nc.scalar.copy, wor_b, wor_raw, slice(P // 2, P))
+        for h in range(HALVES):
+            factors(h)
         for t in range(1, PACK):
             tangents(t)
         nc.vector.quantize_mx(out=wor_q[:].bitcast(FP8X4), scales=wor_s[:], in_=wor_b[:])
-        sum_terms(0)
-        sum_terms(1)
-        weigh(0)
-        last_layer(0)
-        weigh(1)
-        last_layer(1)
-        add_residual(0, nc.scalar.copy)
-        add_residual(1, nc.vector.tensor_copy)
-        quantise_y(0)
-        quantise_y(1)
-        for q in range(4):
+        for h in range(HALVES):
+            sum_terms(h)
+        sums = [last_layer(h) for h in range(HALVES)]
+        add_residual(0, sums[0], nc.scalar.copy)
+        add_residual(1, sums[1], nc.vector.tensor_copy)
+        for h in range(HALVES):
+            quantise_out(h)
+        for q in range(QUADS):
             queue = nc.scalar if q % 2 else nc.sync
-            queue.dma_start(out=out_2[0, 4 * q : 4 * q + 4, :].bitcast(I32),
-                            in_=y_s[32 * q : 32 * q + 4, :].bitcast(I32))
+            queue.dma_start(out=out_2[0, PACK * q : PACK * (q + 1), :].bitcast(I32),
+                            in_=out_s[32 * q : 32 * q + PACK, :].bitcast(I32))

from contextlib import ExitStack

import concourse.mybir as mybir

K, R, F, T, J, M = 512, 512, 512, 2048, 512, 256
FLOPS = 2 * (2 * K * R * J + R * F * M)

F32 = mybir.dt.float32
BF16 = mybir.dt.bfloat16
I32 = mybir.dt.int32
U32 = mybir.dt.uint32
U16 = mybir.dt.uint16
U8 = mybir.dt.uint8
FP8X4 = mybir.dt.float8_e4m3fn_x4
ACT = mybir.ActivationFunctionType
MULT = mybir.AluOpType.mult
ADD = mybir.AluOpType.add

P = 128
PACK = 4
QUADS = 4
PER_COLUMN = 16
DTAB_ROW = 4
W1_ON_SCALAR = 96
HALVES = 2
MH = M // HALVES
LINE = 4
FIRST_LAYER_BANKS = 6


def tile_attend_tlikeness_o_pl_kernel(tc, dtab_words, dtab_scales, tab_words, tab_scales, w1, soft, rs, wor, res,
                                       offs, offs2, offs3, out_0, out_1, out_2):
    nc = tc.nc
    with ExitStack() as ctx:
        sb = ctx.enter_context(tc.tile_pool(name="sb", bufs=1))
        ps1 = ctx.enter_context(tc.psum_pool(name="ps1", bufs=FIRST_LAYER_BANKS))
        ps2 = ctx.enter_context(tc.psum_pool(name="ps2", bufs=HALVES))
        tag_of = {}

        def tile(name, shape, dtype, after=None):
            tag = tag_of.get(after, name)
            tag_of.setdefault(name, tag)
            return sb.tile(shape, dtype, name=name, tag=tag, align_bytes=64)

        def words_view(words):
            return words[0].rearrange("p n t -> p (n t)").bitcast(I32)

        def load_scales(dst, scales, row):
            for q in range(QUADS):
                nc.sync.dma_start(out=dst[32 * q + row : 32 * q + row + PACK, :].bitcast(I32),
                                  in_=scales[0, PACK * q : PACK * (q + 1), :].bitcast(I32))

        def load_weight(name, weight, after=None):
            raw = tile(name, [P, PACK, weight.shape[1]], F32, after)
            nc.sync.dma_start(out=raw[:], in_=weight.rearrange("(p j) c -> p j c", j=PACK))
            return raw

        def deal(copy, dst, raw, groups):
            copy(dst[:].rearrange("p (t i j) -> p i j t", t=PACK, j=PACK)[:, groups],
                 raw[:].rearrange("p j (i t) -> p i j t", t=PACK)[:, groups])

        list1 = tile("list1", [P, J // PER_COLUMN], U16)
        list2 = tile("list2", [P, M // PER_COLUMN], U16)
        list3 = tile("list3", [P, M // PER_COLUMN], U16)
        tab_s = tile("tab_s", [P, T], U8)
        soft_sb = tile("soft_sb", [P, PACK], F32)
        rs_sb = tile("rs_sb", [P, PACK], F32)
        ln_in = tile("ln_in", [P, 1], F32)
        ln_bias = tile("ln_bias", [P, 1], F32)
        zero = tile("zero", [P, 1], F32)

        nc.gpsimd.memset(ln_in[:], 0.0)
        nc.gpsimd.memset(ln_bias[:], 1.0)
        nc.gpsimd.memset(tab_s[:].bitcast(I32), 0)
        nc.gpsimd.dma_start(out=soft_sb[:], in_=soft.rearrange("(p t) o -> p (t o)", t=PACK))
        nc.gpsimd.dma_start(out=rs_sb[:], in_=rs.rearrange("(p t) o -> p (t o)", t=PACK))

        nc.sync.dma_start(out=list1[:], in_=offs)
        w1_raw = load_weight("w1_raw", w1)
        nc.sync.dma_start(out=list3[:], in_=offs3)
        nc.sync.dma_start(out=list2[:], in_=offs2)
        load_scales(tab_s, tab_scales, 0)
        nc.scalar.activation(zero[:], ln_in[:], ACT.Ln, bias=ln_bias[:])
        tab_w = tile("tab_w", [P, T], U32, after="ln_in")
        dtab_s = tile("dtab_s", [P, T], U8, after="ln_bias")
        nc.sync.dma_start(out=tab_w[:].bitcast(I32), in_=words_view(tab_words))
        nc.vector.memset(dtab_s[:].bitcast(I32), 0)
        load_scales(dtab_s, dtab_scales, DTAB_ROW)

        coef = tile("coef", [P, PACK], F32)
        nc.gpsimd.tensor_tensor(coef[:], soft_sb[:], rs_sb[:], MULT)

        g_tab_s = tile("g_tab_s", [P, J], U8)
        g_tab_w = tile("g_tab_w", [P, J], U32)
        g_dtab_w = tile("g_dtab_w", [P, J], U32)
        nc.vector.tensor_copy(g_tab_s[:], tab_s[:].indirect(list1[:]))

        w1_b = tile("w1_b", [P, R * PACK], BF16)
        w1_q = tile("w1_q", [P, R], U32)
        w1_s = tile("w1_s", [P, R], U8, after="tab_s")
        deal(nc.scalar.copy, w1_b, w1_raw, slice(0, W1_ON_SCALAR))
        deal(nc.vector.tensor_copy, w1_b, w1_raw, slice(W1_ON_SCALAR, P))
        dtab_w = tile("dtab_w", [P, T], U32, after="w1_raw")
        nc.sync.dma_start(out=dtab_w[:].bitcast(I32), in_=words_view(dtab_words))
        nc.vector.quantize_mx(out=w1_q[:].bitcast(FP8X4), scales=w1_s[:], in_=w1_b[:])
        wor_raw = load_weight("wor_raw", wor, after="w1_b")

        def first_layer(whole, t, words, scales, row, slots):
            cols = slice(t * P, (t + 1) * P)
            acc = ps1.tile([P, slots.stop - slots.start], F32, name="acc1")
            nc.tensor.matmul_mx(out=acc[:], lhsT=w1_q[:, cols].bitcast(FP8X4), lhsT_scale=w1_s[:, cols],
                                rhs=words[:, slots].bitcast(FP8X4), rhs_scale=scales[row:P, slots],
                                start=True, stop=True)
            nc.scalar.copy(whole[:, slots], acc[:])

        a = [tile("a%d" % t, [P, J], F32) for t in range(PACK)]
        ta = [tile("ta%d" % t, [P, J], F32) for t in range(PACK)]
        slot_halves = [slice(0, J // 2), slice(J // 2, J)]
        for slots in slot_halves:
            entries = slice(slots.start // PER_COLUMN, slots.stop // PER_COLUMN)
            nc.vector.tensor_copy(g_tab_w[:, slots], tab_w[:].indirect(list1[:, entries]))
        for slots in slot_halves:
            first_layer(a[0], 0, g_tab_w, g_tab_s, 0, slots)
        for t in range(1, PACK):
            first_layer(a[t], t, g_tab_w, g_tab_s, 0, slice(0, J))
        res_sb = tile("res_sb", [P, PACK, M], F32, after="g_tab_w")
        nc.sync.dma_start(out=res_sb[:], in_=res.rearrange("(p t) m -> p t m", t=PACK))
        g_dtab_s = tile("g_dtab_s", [P, J], U8, after="tab_w")
        nc.vector.tensor_copy(g_dtab_s[:], dtab_s[:].indirect(list1[:]))

        last = PACK - 1
        uv_first = tile("uv_first", [P, 2, M], F32, after="dtab_s")
        u = [uv_first[:, 0, :]]
        v = [uv_first[:, 1, :]]
        square = [tile("square_first", [P, M], F32, after="g_tab_s")[:]]
        prod = [tile("prod%d" % t, [P, M], F32) for t in range(PACK)]
        log_n2sq = tile("log_n2sq", [P, PACK, M], F32)

        def look_up(t):
            nc.vector.tensor_copy(v[t], a[t][:].indirect(list3[:]))
            nc.vector.tensor_copy(u[t], a[t][:].indirect(list2[:]))

        def product(t, engine):
            engine.tensor_tensor(prod[t][:], u[t], v[t], MULT)

        def log_norm(t):
            nc.scalar.activation(square[t], prod[t][:], ACT.Square)
            nc.scalar.activation(log_n2sq[:, t, :], square[t], ACT.Ln, bias=soft_sb[:, t : t + 1])

        look_up(0)
        product(0, nc.gpsimd)
        nc.vector.tensor_copy(g_dtab_w[:], dtab_w[:].indirect(list1[:]))
        uv_rest = tile("uv_rest", [P, 2, last, M], F32, after="dtab_w")
        u.extend([uv_rest[:, 0, i, :] for i in range(last)])
        v.extend([uv_rest[:, 1, i, :] for i in range(last)])
        for t in range(PACK):
            first_layer(ta[t], t, g_dtab_w, g_dtab_s, DTAB_ROW, slice(0, J))
        for t in range(1, last):
            look_up(t)
            product(t, nc.gpsimd)
        look_up(last)

        square_rest = tile("square_rest", [P, last, M], F32, after="g_dtab_w")
        square.extend([square_rest[:, i, :] for i in range(last)])
        for t in range(last):
            log_norm(t)
        wor_b = tile("wor_b", [P, F * PACK], BF16, after="w1_q")
        wor_q = tile("wor_q", [P, F], U32)
        wor_s = tile("wor_s", [P, F], U8)

        halves = [slice(h * MH, (h + 1) * MH) for h in range(HALVES)]
        du_v = tile("du_v", [P, PACK, M], F32)
        dv_u = tile("dv_u", [P, PACK, M], F32)
        power = tile("power", [P, PACK, M], F32)
        factor = tile("factor", [P, PACK, M], F32)
        dprod = [tile("dprod%d" % h, [P, PACK, MH], F32) for h in range(HALVES)]
        fo_b = [tile("fo_b%d" % h, [P, MH * PACK], BF16) for h in range(HALVES)]
        fo_q = [tile("fo_q%d" % h, [P, MH], U32) for h in range(HALVES)]
        fo_s = [tile("fo_s%d" % h, [P, MH], U8) for h in range(HALVES)]
        out_f = [tile("out_f%d" % h, [P, PACK, MH], F32) for h in range(HALVES)]
        out_b = [tile("out_b%d" % h, [P, MH * PACK], BF16) for h in range(HALVES)]
        out_q = [tile("out_q%d" % h, [P, MH], U32) for h in range(HALVES)]
        out_s = tile("out_s", [P, M], U8)
        out_rows = out_0.rearrange("(p t) m -> p t m", t=PACK)
        out_words = words_view(out_1)

        def by_tile(ap):
            return ap.rearrange("p t (c i) -> p c t i", i=LINE)

        def woven(ap):
            return ap.rearrange("p (c i t) -> p c t i", i=LINE, t=PACK)

        def tangents(t):
            nc.vector.tensor_tensor(du_v[:, t, :], ta[t][:].indirect(list2[:]), v[t], MULT)
            nc.vector.tensor_tensor(dv_u[:, t, :], ta[t][:].indirect(list3[:]), u[t], MULT)

        def factors(h):
            nc.scalar.activation(power[:, :, halves[h]], log_n2sq[:, :, halves[h]], ACT.Exp, bias=zero[:], scale=-1.5)
            for t in range(PACK):
                nc.scalar.activation(factor[:, t, halves[h]], power[:, t, halves[h]], ACT.Copy,
                                     scale=coef[:, t : t + 1])

        def sum_terms(h):
            nc.vector.tensor_tensor(dprod[h][:], du_v[:, :, halves[h]], dv_u[:, :, halves[h]], ADD)

        def last_layer(h):
            nc.vector.tensor_tensor(woven(fo_b[h][:]), by_tile(dprod[h][:]), by_tile(factor[:, :, halves[h]]), MULT)
            nc.vector.quantize_mx(out=fo_q[h][:].bitcast(FP8X4), scales=fo_s[h][:], in_=fo_b[h][:])
            acc = ps2.tile([P, PACK, MH], F32, name="acc2")
            for t in range(PACK):
                cols = slice(t * P, (t + 1) * P)
                nc.tensor.matmul_mx(out=acc[:, t, :], lhsT=wor_q[:, cols].bitcast(FP8X4), lhsT_scale=wor_s[:, cols],
                                    rhs=fo_q[h][:].bitcast(FP8X4), rhs_scale=fo_s[h][:], start=True, stop=True)
            return acc

        def add_residual(h, acc, copy):
            nc.vector.tensor_tensor(out_f[h][:], acc[:], res_sb[:, :, halves[h]], ADD)
            nc.sync.dma_start(out=out_rows[:, :, halves[h]], in_=out_f[h][:])
            copy(woven(out_b[h][:]), by_tile(out_f[h][:]))

        def quantise_out(h):
            nc.vector.quantize_mx(out=out_q[h][:].bitcast(FP8X4), scales=out_s[:, halves[h]], in_=out_b[h][:])
            nc.sync.dma_start(out=out_words[:, halves[h]], in_=out_q[h][:].bitcast(I32))

        tangents(0)
        deal(nc.scalar.copy, wor_b, wor_raw, slice(0, P // 2))
        product(last, nc.vector)
        log_norm(last)
        deal(nc.scalar.copy, wor_b, wor_raw, slice(P // 2, P))
        for h in range(HALVES):
            factors(h)
        for t in range(1, PACK):
            tangents(t)
        nc.vector.quantize_mx(out=wor_q[:].bitcast(FP8X4), scales=wor_s[:], in_=wor_b[:])
        for h in range(HALVES):
            sum_terms(h)
        sums = [last_layer(h) for h in range(HALVES)]
        add_residual(0, sums[0], nc.scalar.copy)
        add_residual(1, sums[1], nc.vector.tensor_copy)
        for h in range(HALVES):
            quantise_out(h)
        for q in range(QUADS):
            queue = nc.scalar if q % 2 else nc.sync
            queue.dma_start(out=out_2[0, PACK * q : PACK * (q + 1), :].bitcast(I32),
                            in_=out_s[32 * q : 32 * q + PACK, :].bitcast(I32))
